import numpy as np
import ml_dtypes


def mxq(x, axis, fmt="e4m3"):
    dtype, down = {"e4m3": (ml_dtypes.float8_e4m3fn, 7), "e5m2": (ml_dtypes.float8_e5m2, 14)}[fmt]
    v = np.moveaxis(np.asarray(x, np.float32).astype(ml_dtypes.bfloat16).astype(np.float64), axis, -1)
    blocks = v.reshape(v.shape[:-1] + (-1, 32))
    amax = np.abs(blocks).max(-1, keepdims=True)
    byte = np.maximum(np.where(amax > 0, np.frexp(amax)[1] - 1 + 127, 0) - down, 1)
    scale = np.exp2(byte - 127.0)
    codes = (blocks / scale).astype(np.float32).astype(dtype).astype(np.float64)
    return np.moveaxis((codes * scale).reshape(v.shape), -1, axis)


WIDE = False


def mx_kscale(k):
    if not WIDE:
        return np.ones(k)
    levels = np.array([30, -30])
    if k % 512:
        return np.exp2(np.random.permutation(np.resize(levels, k // 32))).repeat(32)
    a = np.empty((k // 512, 16))
    for p in range(k // 512):
        a[p, :8] = np.random.permutation(np.resize(levels, 8))
        for g in range(8):
            far = levels[np.abs(levels - a[p, g]) >= 10]
            a[p, g + 8] = far[np.random.randint(len(far))]
    return np.exp2(a.ravel()).repeat(32)


def f64(x):
    return np.asarray(x).astype(np.float64)


def striped(idx):
    return np.tile(np.asarray(idx).reshape(-1, 16).T, (8, 1)).astype(np.uint16)


def unstriped(offs):
    return offs[:16].T.reshape(-1).astype(np.int64)


E2M1 = np.array([0.0, 0.5, 1.0, 1.5, 2.0, 3.0, 4.0, 6.0, -0.0, -0.5, -1.0, -1.5, -2.0, -3.0, -4.0, -6.0])


def pack_weight(w, fmt):
    k, n = w.shape
    w = f64(np.asarray(w, np.float32).astype(ml_dtypes.bfloat16)).reshape(k // 32, 32, n)
    amax = np.abs(w).max(1)
    if fmt in ("e4m3", "e5m2"):
        byte = np.frexp(amax)[1] - 1 + 127 - (7 if fmt == "e4m3" else 14)
    else:
        mant, ex = np.frexp(amax / 6.0)
        byte = np.where(mant > 0.5, ex, ex - 1) + 127
    byte = np.clip(np.where(amax > 0, byte, 1), 1, 254)
    scaled = (w * np.exp2(127.0 - byte)[:, None, :]).reshape(k, n).astype(np.float32)
    by_word = np.ascontiguousarray(scaled.reshape(k // 512, 128, 4, n).transpose(0, 1, 3, 2))
    if fmt in ("e4m3", "e5m2"):
        words = by_word.astype(ml_dtypes.float8_e4m3fn if fmt == "e4m3" else ml_dtypes.float8_e5m2).view(np.uint8)
    else:
        c = by_word.astype(ml_dtypes.float4_e2m1fn).view(np.uint8) & 0xF
        words = (c[..., 0::2] | (c[..., 1::2] << 4)).reshape(k // 512, 128, 2 * n)
    return np.ascontiguousarray(words), np.ascontiguousarray(byte.astype(np.uint8).reshape(k // 512, 16, n))


def unpack_weight(words, scales, fmt):
    g, _, n = scales.shape
    words = np.ascontiguousarray(words).reshape(g, 128, n, -1)
    if fmt in ("e4m3", "e5m2"):
        vals = words.view(ml_dtypes.float8_e4m3fn if fmt == "e4m3" else ml_dtypes.float8_e5m2).astype(np.float64)
    else:
        nib = np.empty((g, 128, n, 4), np.uint8)
        nib[..., 0::2] = words & 0xF
        nib[..., 1::2] = words >> 4
        vals = E2M1[nib]
    vals = vals * np.repeat(np.exp2(scales.astype(np.float64) - 127.0), 8, axis=1)[..., None]
    return vals.transpose(0, 1, 3, 2).reshape(g * 512, n)


def e4m3fn_bytes(y):
    return np.clip(np.asarray(y, np.float64), -448.0, 448.0).astype(np.float32).astype(ml_dtypes.float8_e4m3fn).view(np.uint8)


def e4m3fn_values(b):
    return np.asarray(b, np.uint8).view(ml_dtypes.float8_e4m3fn).astype(np.float64)


K, T, V, J, R, N = 512, 1024, 2048, 256, 512, 256


def setup_inputs():
    n = np.random.standard_normal
    idx = np.random.permutation(V)[:R]
    idx2 = np.random.permutation(V)[:R]
    idx3 = np.random.permutation(T)[:J]
    fk = mx_kscale(K)
    fr = mx_kscale(R)
    xtp = pack_weight(n((K, T)) / fk[:, None], "e5m2")
    wbp = pack_weight(n((R, N)) * 1 / np.sqrt(R) / fr[:, None], "e2m1")
    return {
        "xt_words": xtp[0],
        "xt_scales": xtp[1],
        "ca": e4m3fn_bytes(60.0 * n((K, V))),
        "sa": (np.random.uniform(0.0004, 0.0012, (K, 1)) * fk[:, None]).astype(np.float32),
        "sb": (np.random.uniform(0.0004, 0.0012, (K, 1)) * fk[:, None]).astype(np.float32),
        "sr": (np.random.uniform(0.5, 1.6, (R, 1)) * fr[:, None]).astype(np.float32),
        "wb_words": wbp[0],
        "wb_scales": wbp[1],
        "offs": striped(idx),
        "offs2": striped(idx2),
        "offs3": striped(idx3),
    }


def reference(xt_words, xt_scales, ca, sa, sb, sr, wb_words, wb_scales, offs, offs2, offs3):
    idx = unstriped(offs)
    idx2 = unstriped(offs2)
    idx3 = unstriped(offs3)
    xtu = unpack_weight(xt_words, xt_scales, "e5m2")
    wbu = unpack_weight(wb_words, wb_scales, "e2m1")
    wa = e4m3fn_values(ca)[:, idx] * f64(sa)
    wc = e4m3fn_values(ca)[:, idx2] * f64(sb)
    waq = mxq(wa, 0, "e4m3")
    xtidx3g = xtu[:, idx3]
    a = waq.T @ xtidx3g
    wcq = mxq(wc, 0, "e4m3")
    b = wcq.T @ xtidx3g
    hid = np.maximum(a, b) * f64(sr)
    hidq = mxq(hid, 0, "e4m3")
    p = wbu.T @ hidq
    return p

@@ -1,0 +1,179 @@
+from contextlib import ExitStack
+
+import concourse.mybir as mybir
+
+K, T, V, J, R, N = 512, 1024, 2048, 256, 512, 256
+FLOPS = 2 * (2 * K * R * J + R * N * J)
+
+F32 = mybir.dt.float32
+BF16 = mybir.dt.bfloat16
+I32 = mybir.dt.int32
+U32 = mybir.dt.uint32
+U16 = mybir.dt.uint16
+U8 = mybir.dt.uint8
+FP8 = mybir.dt.float8_e4m3fn
+E4M3X4 = mybir.dt.float8_e4m3fn_x4
+E5M2X4 = mybir.dt.float8_e5m2_x4
+E2M1X4 = mybir.dt.float4_e2m1fn_x4
+COPY = mybir.ActivationFunctionType.Copy
+ALU = mybir.AluOpType
+
+P = 128
+PACK = 4
+JH = 128
+A_PIECES = 4
+B_SCALAR_M = 64
+JS = 96
+
+
+def tile_list_rivalcolumns_kernel(tc, xt_words, xt_scales, ca, sa, sb, sr, wb_words, wb_scales, offs, offs2, offs3, out):
+    nc = tc.nc
+    with ExitStack() as ctx:
+        keep = ctx.enter_context(tc.tile_pool(name="keep", bufs=1))
+        psum = ctx.enter_context(tc.psum_pool(name="psum", bufs=1))
+
+        def sb_tile(name, shape, dtype):
+            return keep.tile(shape, dtype, name=name, align_bytes=64)
+
+        list_a = sb_tile("list_a", [P, R // 16], U16)
+        list_b = sb_tile("list_b", [P, R // 16], U16)
+        list_x = sb_tile("list_x", [P, J // 16], U16)
+        table = [sb_tile("table%d" % t, [P, V], U8) for t in range(PACK)]
+        step_a = sb_tile("step_a", [P, PACK], F32)
+        step_b = sb_tile("step_b", [P, PACK], F32)
+        gain = sb_tile("gain", [P, PACK], F32)
+        x_all = sb_tile("x_all", [P, T], I32)
+        xs_all = sb_tile("xs_all", [P, T], U8)
+        wb_w = sb_tile("wb_w", [P, 2 * N], U8)
+        wb_s = sb_tile("wb_s", [P, N], U8)
+
+        nc.vector.memset(xs_all[:].bitcast(I32), 0)
+        nc.vector.memset(wb_s[:].bitcast(I32), 0)
+
+        ca_rows = ca.rearrange("(p t) v -> t p v", t=PACK)
+        nc.sync.dma_start(list_a[:], offs)
+        nc.sync.dma_start(table[0][:], ca_rows[0])
+        nc.sync.dma_start(step_a[:], sa.rearrange("(p t) o -> p (t o)", t=PACK))
+        for t in range(1, PACK):
+            nc.sync.dma_start(table[t][:], ca_rows[t])
+        nc.sync.dma_start(list_b[:], offs2)
+        nc.sync.dma_start(step_b[:], sb.rearrange("(p t) o -> p (t o)", t=PACK))
+        nc.sync.dma_start(x_all[:], xt_words[0].rearrange("p c t -> p (c t)").bitcast(I32))
+        nc.sync.dma_start(list_x[:], offs3)
+        for q in range(4):
+            nc.sync.dma_start(xs_all[32 * q : 32 * q + 4, :].bitcast(I32), xt_scales[0, 4 * q : 4 * q + 4, :].bitcast(I32))
+        nc.sync.dma_start(gain[:], sr.rearrange("(p t) o -> p (t o)", t=PACK))
+        nc.sync.dma_start(wb_w[:].bitcast(I32), wb_words[0].bitcast(I32))
+        for q in range(4):
+            nc.sync.dma_start(wb_s[32 * q : 32 * q + 4, :].bitcast(I32), wb_scales[0, 4 * q : 4 * q + 4, :].bitcast(I32))
+
+        picked_a = [sb_tile("picked_a%d" % t, [P, R], U8) for t in range(PACK)]
+        picked_b = [sb_tile("picked_b%d" % t, [P, R], U8) for t in range(PACK)]
+        rows_a = sb_tile("rows_a", [P, PACK, R], BF16)
+        rows_b = sb_tile("rows_b", [P, PACK, R], BF16)
+        woven_a = sb_tile("woven_a", [P, PACK * R], BF16)
+        woven_b = sb_tile("woven_b", [P, PACK * R], BF16)
+
+        def gather(picked, lst, t):
+            nc.vector.tensor_copy(picked[t][:], table[t][:].indirect(lst[:]))
+
+        def scale(rows, picked, step, t):
+            nc.scalar.activation(out=rows[:, t, :], in_=picked[t][:].bitcast(FP8), func=COPY, scale=step[:, t : t + 1])
+
+        def weave_views(woven, rows, m0, m1, u0=0, u1=PACK):
+            dst = woven[:].rearrange("p (u m t) -> p m t u", u=PACK, t=PACK)[:, m0:m1, :, u0:u1]
+            src = rows[:].rearrange("p t (m u) -> p m t u", u=PACK)[:, m0:m1, :, u0:u1]
+            return dst, src
+
+        for t in range(PACK):
+            gather(picked_a, list_a, t)
+            scale(rows_a, picked_a, step_a, t)
+        piece = P // A_PIECES
+        for t in range(PACK):
+            gather(picked_b, list_b, t)
+            dst, src = weave_views(woven_a, rows_a, t * piece, (t + 1) * piece)
+            nc.scalar.copy(out=dst, in_=src)
+            scale(rows_b, picked_b, step_b, t)
+
+        x_w = sb_tile("x_w", [P, J], U32)
+        x_s = sb_tile("x_s", [P, J], U8)
+        nc.vector.tensor_copy(x_w[:], x_all[:].bitcast(U32).indirect(list_x[:]))
+        nc.vector.tensor_copy(x_s[:], xs_all[:].indirect(list_x[:]))
+
+        wa_w = [sb_tile("wa_w%d" % g, [P, 2 * P], U32) for g in range(2)]
+        wa_s = [sb_tile("wa_s%d" % g, [P, 2 * P], U8) for g in range(2)]
+        for g in range(2):
+            nc.vector.quantize_mx(out=wa_w[g][:].bitcast(E4M3X4), scales=wa_s[g][:], in_=woven_a[:, g * 1024 : (g + 1) * 1024])
+
+        dst, src = weave_views(woven_b, rows_b, 0, B_SCALAR_M)
+        nc.scalar.copy(out=dst, in_=src)
+        for g in range(2):
+            dst, src = weave_views(woven_b, rows_b, B_SCALAR_M, P, 2 * g, 2 * g + 2)
+            nc.vector.tensor_copy(out=dst, in_=src)
+
+        def first_stage(dst, w, s, i):
+            nc.tensor.matmul_mx(
+                out=dst,
+                lhsT=w[:, i * P : (i + 1) * P].bitcast(E4M3X4), lhsT_scale=s[:, i * P : (i + 1) * P],
+                rhs=x_w[:].bitcast(E5M2X4), rhs_scale=x_s[:],
+                start=True, stop=True,
+            )
+
+        halves = J // JH
+        a_ps = [psum.tile([P, 2, J], F32, name="a_ps%d" % g, tag="pair%d" % g) for g in range(2)]
+        b_ps = [psum.tile([P, J], F32, name="b_ps%d" % u) for u in range(PACK)]
+        a_sb = [sb_tile("a_sb%d" % g, [P, 2, J], F32) for g in range(2)]
+        for g in range(2):
+            for i in range(2):
+                first_stage(a_ps[g][:, i, :], wa_w[g][:], wa_s[g][:], i)
+            nc.scalar.copy(out=a_sb[g][:], in_=a_ps[g][:])
+
+        wc_w = [sb_tile("wc_w%d" % g, [P, 2 * P], U32) for g in range(2)]
+        wc_s = [sb_tile("wc_s%d" % g, [P, 2 * P], U8) for g in range(2)]
+        for g in range(2):
+            nc.vector.quantize_mx(out=wc_w[g][:].bitcast(E4M3X4), scales=wc_s[g][:], in_=woven_b[:, g * 1024 : (g + 1) * 1024])
+            for i in range(2):
+                first_stage(b_ps[2 * g + i][:], wc_w[g][:], wc_s[g][:], i)
+
+        top = sb_tile("top", [P, PACK, J], F32)
+        hid = [sb_tile("hid%d" % h, [P, JH, PACK], BF16) for h in range(halves)]
+        hid_rows = sb_tile("hid_rows", [P, PACK, JS], BF16)
+        hid_w = [sb_tile("hid_w%d" % h, [P, JH], U32) for h in range(halves)]
+        hid_s = [sb_tile("hid_s%d" % h, [P, JH], U8) for h in range(halves)]
+
+        def larger(u, j0, j1):
+            nc.vector.tensor_tensor(out=top[:, u, j0:j1], in0=b_ps[u][:, j0:j1], in1=a_sb[u // 2][:, u % 2, j0:j1], op=ALU.max)
+
+        def weigh(dst, j0, j1):
+            nc.vector.tensor_tensor(out=dst, in0=top[:, :, j0:j1].rearrange("p u j -> p j u"), in1=gain[:].unsqueeze(1).to_broadcast([P, j1 - j0, PACK]), op=ALU.mult)
+
+        for u in range(PACK):
+            if u < PACK - 1:
+                larger(u, 0, J)
+            else:
+                larger(u, JH, J)
+                larger(u, 0, JH)
+            nc.scalar.activation(out=hid_rows[:, u, :], in_=top[:, u, 0:JS], func=COPY, scale=gain[:, u : u + 1])
+        weigh(hid[1][:], JH, J)
+        weigh(hid[0][:, JS:JH, :], JS, JH)
+        nc.scalar.copy(out=hid[0][:, 0:JS, :], in_=hid_rows[:].rearrange("p u j -> p j u"))
+        for h in (1, 0):
+            nc.vector.quantize_mx(out=hid_w[h][:].bitcast(E4M3X4), scales=hid_s[h][:], in_=hid[h][:].rearrange("p j u -> p (j u)"))
+
+        for h in (1, 0):
+            for c in range(N // P):
+                o_ps = psum.tile([P, JH], F32, name="o_ps%d%d" % (h, c), tag=("pair%d" if h == 0 else "out%d") % c)
+                nc.tensor.matmul_mx(
+                    out=o_ps[:],
+                    lhsT=wb_w[:, 2 * c * P : 2 * (c + 1) * P].bitcast(E2M1X4), lhsT_scale=wb_s[:, c * P : (c + 1) * P],
+                    rhs=hid_w[h][:].bitcast(E4M3X4), rhs_scale=hid_s[h][:],
+                    start=True, stop=True,
+                )
+                o_sb = sb_tile("o_sb%d%d" % (h, c), [P, JH], F32)
+                dst = out[c * P : (c + 1) * P, h * JH : (h + 1) * JH]
+                if c == 0:
+                    nc.scalar.copy(out=o_sb[:], in_=o_ps[:])
+                    nc.scalar.dma_start(dst, o_sb[:])
+                else:
+                    nc.vector.tensor_copy(out=o_sb[:], in_=o_ps[:])
+                    nc.sync.dma_start(dst, o_sb[:])

@@ -22,7 +22,7 @@ P = 128
 PACK = 4
 JH = 128
 A_PIECES = 4
-B_SCALAR_M = 64
+B_SCALAR_M = 48
 JS = 96
 
 
@@ -51,8 +51,8 @@ def tile_list_rivalcolumns_kernel(tc, xt_words, xt_scales, ca, sa, sb, sr, wb_wo
         nc.vector.memset(wb_s[:].bitcast(I32), 0)
 
         ca_rows = ca.rearrange("(p t) v -> t p v", t=PACK)
-        nc.sync.dma_start(list_a[:], offs)
         nc.sync.dma_start(table[0][:], ca_rows[0])
+        nc.sync.dma_start(list_a[:], offs)
         nc.sync.dma_start(step_a[:], sa.rearrange("(p t) o -> p (t o)", t=PACK))
         for t in range(1, PACK):
             nc.sync.dma_start(table[t][:], ca_rows[t])

@@ -145,7 +145,12 @@ def tile_list_rivalcolumns_kernel(tc, xt_words, xt_scales, ca, sa, sb, sr, wb_wo
             nc.vector.tensor_tensor(out=top[:, u, j0:j1], in0=b_ps[u][:, j0:j1], in1=a_sb[u // 2][:, u % 2, j0:j1], op=ALU.max)
 
         def weigh(dst, j0, j1):
-            nc.vector.tensor_tensor(out=dst, in0=top[:, :, j0:j1].rearrange("p u j -> p j u"), in1=gain[:].unsqueeze(1).to_broadcast([P, j1 - j0, PACK]), op=ALU.mult)
+            nc.vector.tensor_tensor(
+                out=dst.rearrange("p (c i) u -> p c u i", i=4),
+                in0=top[:, :, j0:j1].rearrange("p u (c i) -> p c u i", i=4),
+                in1=gain[:].unsqueeze(1).unsqueeze(3).to_broadcast([P, (j1 - j0) // 4, PACK, 4]),
+                op=ALU.mult,
+            )
 
         for u in range(PACK):
             if u < PACK - 1:
@@ -156,7 +161,7 @@ def tile_list_rivalcolumns_kernel(tc, xt_words, xt_scales, ca, sa, sb, sr, wb_wo
             nc.scalar.activation(out=hid_rows[:, u, :], in_=top[:, u, 0:JS], func=COPY, scale=gain[:, u : u + 1])
         weigh(hid[1][:], JH, J)
         weigh(hid[0][:, JS:JH, :], JS, JH)
-        nc.scalar.copy(out=hid[0][:, 0:JS, :], in_=hid_rows[:].rearrange("p u j -> p j u"))
+        nc.scalar.copy(out=hid[0][:, 0:JS, :].rearrange("p (c i) u -> p c u i", i=4), in_=hid_rows[:].rearrange("p u (c i) -> p c u i", i=4))
         for h in (1, 0):
             nc.vector.quantize_mx(out=hid_w[h][:].bitcast(E4M3X4), scales=hid_s[h][:], in_=hid[h][:].rearrange("p j u -> p (j u)"))
 

@@ -22,7 +22,7 @@ P = 128
 PACK = 4
 JH = 128
 A_PIECES = 4
-B_SCALAR_M = 48
+B_SCALAR_M = 60
 JS = 96
 
 
@@ -74,26 +74,41 @@ def tile_list_rivalcolumns_kernel(tc, xt_words, xt_scales, ca, sa, sb, sr, wb_wo
         woven_a = sb_tile("woven_a", [P, PACK * R], BF16)
         woven_b = sb_tile("woven_b", [P, PACK * R], BF16)
 
-        def gather(picked, lst, t):
-            nc.vector.tensor_copy(picked[t][:], table[t][:].indirect(lst[:]))
+        def gather(dst, lst, t, r0, r1):
+            nc.vector.tensor_copy(dst, table[t][:].indirect(lst[:, r0 // 16 : r1 // 16]))
 
-        def scale(rows, picked, step, t):
-            nc.scalar.activation(out=rows[:, t, :], in_=picked[t][:].bitcast(FP8), func=COPY, scale=step[:, t : t + 1])
+        def scale(rows, src, step, t, r0, r1):
+            nc.scalar.activation(out=rows[:, t, r0:r1], in_=src.bitcast(FP8), func=COPY, scale=step[:, t : t + 1])
 
         def weave_views(woven, rows, m0, m1, u0=0, u1=PACK):
             dst = woven[:].rearrange("p (u m t) -> p m t u", u=PACK, t=PACK)[:, m0:m1, :, u0:u1]
             src = rows[:].rearrange("p t (m u) -> p m t u", u=PACK)[:, m0:m1, :, u0:u1]
             return dst, src
 
-        for t in range(PACK):
-            gather(picked_a, list_a, t)
-            scale(rows_a, picked_a, step_a, t)
         piece = P // A_PIECES
-        for t in range(PACK):
-            gather(picked_b, list_b, t)
-            dst, src = weave_views(woven_a, rows_a, t * piece, (t + 1) * piece)
+        H = R // 2
+
+        def weave_a(i):
+            dst, src = weave_views(woven_a, rows_a, i * piece, (i + 1) * piece)
             nc.scalar.copy(out=dst, in_=src)
-            scale(rows_b, picked_b, step_b, t)
+
+        for t in range(PACK - 1):
+            gather(picked_a[t][:], list_a, t, 0, R)
+            scale(rows_a, picked_a[t][:], step_a, t, 0, R)
+        gather(picked_a[3][:, 0:H], list_a, 3, 0, H)
+        scale(rows_a, picked_a[3][:, 0 : H // 2], step_a, 3, 0, H // 2)
+        scale(rows_a, picked_a[3][:, H // 2 : H], step_a, 3, H // 2, H)
+        weave_a(0)
+        gather(picked_a[3][:, H:R], list_a, 3, H, R)
+        scale(rows_a, picked_a[3][:, H:R], step_a, 3, H, R)
+        for t in range(PACK):
+            gather(picked_b[t][:], list_b, t, 0, R)
+            if t < PACK - 1:
+                weave_a(t + 1)
+                scale(rows_b, picked_b[t][:], step_b, t, 0, R)
+            else:
+                scale(rows_b, picked_b[t][:, 0:H], step_b, t, 0, H)
+                scale(rows_b, picked_b[t][:, H:R], step_b, t, H, R)
 
         x_w = sb_tile("x_w", [P, J], U32)
         x_s = sb_tile("x_s", [P, J], U8)

from contextlib import ExitStack

import concourse.mybir as mybir

K, T, V, J, R, N = 512, 1024, 2048, 256, 512, 256
FLOPS = 2 * (2 * K * R * J + R * N * J)

F32 = mybir.dt.float32
BF16 = mybir.dt.bfloat16
I32 = mybir.dt.int32
U32 = mybir.dt.uint32
U16 = mybir.dt.uint16
U8 = mybir.dt.uint8
FP8 = mybir.dt.float8_e4m3fn
E4M3X4 = mybir.dt.float8_e4m3fn_x4
E5M2X4 = mybir.dt.float8_e5m2_x4
E2M1X4 = mybir.dt.float4_e2m1fn_x4
COPY = mybir.ActivationFunctionType.Copy
ALU = mybir.AluOpType

P = 128
PACK = 4
JH = 128
A_PIECES = 4
B_SCALAR_M = 60
JS = 96


def tile_list_rivalcolumns_kernel(tc, xt_words, xt_scales, ca, sa, sb, sr, wb_words, wb_scales, offs, offs2, offs3, out):
    nc = tc.nc
    with ExitStack() as ctx:
        keep = ctx.enter_context(tc.tile_pool(name="keep", bufs=1))
        psum = ctx.enter_context(tc.psum_pool(name="psum", bufs=1))

        def sb_tile(name, shape, dtype):
            return keep.tile(shape, dtype, name=name, align_bytes=64)

        list_a = sb_tile("list_a", [P, R // 16], U16)
        list_b = sb_tile("list_b", [P, R // 16], U16)
        list_x = sb_tile("list_x", [P, J // 16], U16)
        table = [sb_tile("table%d" % t, [P, V], U8) for t in range(PACK)]
        step_a = sb_tile("step_a", [P, PACK], F32)
        step_b = sb_tile("step_b", [P, PACK], F32)
        gain = sb_tile("gain", [P, PACK], F32)
        x_all = sb_tile("x_all", [P, T], I32)
        xs_all = sb_tile("xs_all", [P, T], U8)
        wb_w = sb_tile("wb_w", [P, 2 * N], U8)
        wb_s = sb_tile("wb_s", [P, N], U8)

        nc.vector.memset(xs_all[:].bitcast(I32), 0)
        nc.vector.memset(wb_s[:].bitcast(I32), 0)

        ca_rows = ca.rearrange("(p t) v -> t p v", t=PACK)
        nc.sync.dma_start(table[0][:], ca_rows[0])
        nc.sync.dma_start(list_a[:], offs)
        nc.sync.dma_start(step_a[:], sa.rearrange("(p t) o -> p (t o)", t=PACK))
        for t in range(1, PACK):
            nc.sync.dma_start(table[t][:], ca_rows[t])
        nc.sync.dma_start(list_b[:], offs2)
        nc.sync.dma_start(step_b[:], sb.rearrange("(p t) o -> p (t o)", t=PACK))
        nc.sync.dma_start(x_all[:], xt_words[0].rearrange("p c t -> p (c t)").bitcast(I32))
        nc.sync.dma_start(list_x[:], offs3)
        for q in range(4):
            nc.sync.dma_start(xs_all[32 * q : 32 * q + 4, :].bitcast(I32), xt_scales[0, 4 * q : 4 * q + 4, :].bitcast(I32))
        nc.sync.dma_start(gain[:], sr.rearrange("(p t) o -> p (t o)", t=PACK))
        nc.sync.dma_start(wb_w[:].bitcast(I32), wb_words[0].bitcast(I32))
        for q in range(4):
            nc.sync.dma_start(wb_s[32 * q : 32 * q + 4, :].bitcast(I32), wb_scales[0, 4 * q : 4 * q + 4, :].bitcast(I32))

        picked_a = [sb_tile("picked_a%d" % t, [P, R], U8) for t in range(PACK)]
        picked_b = [sb_tile("picked_b%d" % t, [P, R], U8) for t in range(PACK)]
        rows_a = sb_tile("rows_a", [P, PACK, R], BF16)
        rows_b = sb_tile("rows_b", [P, PACK, R], BF16)
        woven_a = sb_tile("woven_a", [P, PACK * R], BF16)
        woven_b = sb_tile("woven_b", [P, PACK * R], BF16)

        def gather(dst, lst, t, r0, r1):
            nc.vector.tensor_copy(dst, table[t][:].indirect(lst[:, r0 // 16 : r1 // 16]))

        def scale(rows, src, step, t, r0, r1):
            nc.scalar.activation(out=rows[:, t, r0:r1], in_=src.bitcast(FP8), func=COPY, scale=step[:, t : t + 1])

        def weave_views(woven, rows, m0, m1, u0=0, u1=PACK):
            dst = woven[:].rearrange("p (u m t) -> p m t u", u=PACK, t=PACK)[:, m0:m1, :, u0:u1]
            src = rows[:].rearrange("p t (m u) -> p m t u", u=PACK)[:, m0:m1, :, u0:u1]
            return dst, src

        piece = P // A_PIECES
        H = R // 2

        def weave_a(i):
            dst, src = weave_views(woven_a, rows_a, i * piece, (i + 1) * piece)
            nc.scalar.copy(out=dst, in_=src)

        for t in range(PACK - 1):
            gather(picked_a[t][:], list_a, t, 0, R)
            scale(rows_a, picked_a[t][:], step_a, t, 0, R)
        gather(picked_a[3][:, 0:H], list_a, 3, 0, H)
        scale(rows_a, picked_a[3][:, 0 : H // 2], step_a, 3, 0, H // 2)
        scale(rows_a, picked_a[3][:, H // 2 : H], step_a, 3, H // 2, H)
        weave_a(0)
        gather(picked_a[3][:, H:R], list_a, 3, H, R)
        scale(rows_a, picked_a[3][:, H:R], step_a, 3, H, R)
        for t in range(PACK):
            gather(picked_b[t][:], list_b, t, 0, R)
            if t < PACK - 1:
                weave_a(t + 1)
                scale(rows_b, picked_b[t][:], step_b, t, 0, R)
            else:
                scale(rows_b, picked_b[t][:, 0:H], step_b, t, 0, H)
                scale(rows_b, picked_b[t][:, H:R], step_b, t, H, R)

        x_w = sb_tile("x_w", [P, J], U32)
        x_s = sb_tile("x_s", [P, J], U8)
        nc.vector.tensor_copy(x_w[:], x_all[:].bitcast(U32).indirect(list_x[:]))
        nc.vector.tensor_copy(x_s[:], xs_all[:].indirect(list_x[:]))

        wa_w = [sb_tile("wa_w%d" % g, [P, 2 * P], U32) for g in range(2)]
        wa_s = [sb_tile("wa_s%d" % g, [P, 2 * P], U8) for g in range(2)]
        for g in range(2):
            nc.vector.quantize_mx(out=wa_w[g][:].bitcast(E4M3X4), scales=wa_s[g][:], in_=woven_a[:, g * 1024 : (g + 1) * 1024])

        dst, src = weave_views(woven_b, rows_b, 0, B_SCALAR_M)
        nc.scalar.copy(out=dst, in_=src)
        for g in range(2):
            dst, src = weave_views(woven_b, rows_b, B_SCALAR_M, P, 2 * g, 2 * g + 2)
            nc.vector.tensor_copy(out=dst, in_=src)

        def first_stage(dst, w, s, i):
            nc.tensor.matmul_mx(
                out=dst,
                lhsT=w[:, i * P : (i + 1) * P].bitcast(E4M3X4), lhsT_scale=s[:, i * P : (i + 1) * P],
                rhs=x_w[:].bitcast(E5M2X4), rhs_scale=x_s[:],
                start=True, stop=True,
            )

        halves = J // JH
        a_ps = [psum.tile([P, 2, J], F32, name="a_ps%d" % g, tag="pair%d" % g) for g in range(2)]
        b_ps = [psum.tile([P, J], F32, name="b_ps%d" % u) for u in range(PACK)]
        a_sb = [sb_tile("a_sb%d" % g, [P, 2, J], F32) for g in range(2)]
        for g in range(2):
            for i in range(2):
                first_stage(a_ps[g][:, i, :], wa_w[g][:], wa_s[g][:], i)
            nc.scalar.copy(out=a_sb[g][:], in_=a_ps[g][:])

        wc_w = [sb_tile("wc_w%d" % g, [P, 2 * P], U32) for g in range(2)]
        wc_s = [sb_tile("wc_s%d" % g, [P, 2 * P], U8) for g in range(2)]
        for g in range(2):
            nc.vector.quantize_mx(out=wc_w[g][:].bitcast(E4M3X4), scales=wc_s[g][:], in_=woven_b[:, g * 1024 : (g + 1) * 1024])
            for i in range(2):
                first_stage(b_ps[2 * g + i][:], wc_w[g][:], wc_s[g][:], i)

        top = sb_tile("top", [P, PACK, J], F32)
        hid = [sb_tile("hid%d" % h, [P, JH, PACK], BF16) for h in range(halves)]
        hid_rows = sb_tile("hid_rows", [P, PACK, JS], BF16)
        hid_w = [sb_tile("hid_w%d" % h, [P, JH], U32) for h in range(halves)]
        hid_s = [sb_tile("hid_s%d" % h, [P, JH], U8) for h in range(halves)]

        def larger(u, j0, j1):
            nc.vector.tensor_tensor(out=top[:, u, j0:j1], in0=b_ps[u][:, j0:j1], in1=a_sb[u // 2][:, u % 2, j0:j1], op=ALU.max)

        def weigh(dst, j0, j1):
            nc.vector.tensor_tensor(
                out=dst.rearrange("p (c i) u -> p c u i", i=4),
                in0=top[:, :, j0:j1].rearrange("p u (c i) -> p c u i", i=4),
                in1=gain[:].unsqueeze(1).unsqueeze(3).to_broadcast([P, (j1 - j0) // 4, PACK, 4]),
                op=ALU.mult,
            )

        for u in range(PACK):
            if u < PACK - 1:
                larger(u, 0, J)
            else:
                larger(u, JH, J)
                larger(u, 0, JH)
            nc.scalar.activation(out=hid_rows[:, u, :], in_=top[:, u, 0:JS], func=COPY, scale=gain[:, u : u + 1])
        weigh(hid[1][:], JH, J)
        weigh(hid[0][:, JS:JH, :], JS, JH)
        nc.scalar.copy(out=hid[0][:, 0:JS, :].rearrange("p (c i) u -> p c u i", i=4), in_=hid_rows[:].rearrange("p u (c i) -> p c u i", i=4))
        for h in (1, 0):
            nc.vector.quantize_mx(out=hid_w[h][:].bitcast(E4M3X4), scales=hid_s[h][:], in_=hid[h][:].rearrange("p j u -> p (j u)"))

        for h in (1, 0):
            for c in range(N // P):
                o_ps = psum.tile([P, JH], F32, name="o_ps%d%d" % (h, c), tag=("pair%d" if h == 0 else "out%d") % c)
                nc.tensor.matmul_mx(
                    out=o_ps[:],
                    lhsT=wb_w[:, 2 * c * P : 2 * (c + 1) * P].bitcast(E2M1X4), lhsT_scale=wb_s[:, c * P : (c + 1) * P],
                    rhs=hid_w[h][:].bitcast(E4M3X4), rhs_scale=hid_s[h][:],
                    start=True, stop=True,
                )
                o_sb = sb_tile("o_sb%d%d" % (h, c), [P, JH], F32)
                dst = out[c * P : (c + 1) * P, h * JH : (h + 1) * JH]
                if c == 0:
                    nc.scalar.copy(out=o_sb[:], in_=o_ps[:])
                    nc.scalar.dma_start(dst, o_sb[:])
                else:
                    nc.vector.tensor_copy(out=o_sb[:], in_=o_ps[:])
                    nc.sync.dma_start(dst, o_sb[:])
